import numpy as np
import ml_dtypes


def mxq(x, axis, fmt="e4m3"):
    dtype, down = {"e4m3": (ml_dtypes.float8_e4m3fn, 7), "e5m2": (ml_dtypes.float8_e5m2, 14)}[fmt]
    v = np.moveaxis(np.asarray(x, np.float32).astype(ml_dtypes.bfloat16).astype(np.float64), axis, -1)
    blocks = v.reshape(v.shape[:-1] + (-1, 32))
    amax = np.abs(blocks).max(-1, keepdims=True)
    byte = np.maximum(np.where(amax > 0, np.frexp(amax)[1] - 1 + 127, 0) - down, 1)
    scale = np.exp2(byte - 127.0)
    codes = (blocks / scale).astype(np.float32).astype(dtype).astype(np.float64)
    return np.moveaxis((codes * scale).reshape(v.shape), -1, axis)


WIDE = False


def mx_kscale(k):
    if not WIDE:
        return np.ones(k)
    levels = np.array([10, -10, 5, -5, 0])
    if k % 512:
        return np.exp2(np.random.permutation(np.resize(levels, k // 32))).repeat(32)
    a = np.empty((k // 512, 16))
    for p in range(k // 512):
        a[p, :8] = np.random.permutation(np.resize(levels, 8))
        for g in range(8):
            far = levels[np.abs(levels - a[p, g]) >= 10]
            a[p, g + 8] = far[np.random.randint(len(far))]
    return np.exp2(a.ravel()).repeat(32)


def f64(x):
    return np.asarray(x).astype(np.float64)


def striped(idx):
    return np.tile(np.asarray(idx).reshape(-1, 16).T, (8, 1)).astype(np.uint16)


def unstriped(offs):
    return offs[:16].T.reshape(-1).astype(np.int64)


E2M1 = np.array([0.0, 0.5, 1.0, 1.5, 2.0, 3.0, 4.0, 6.0, -0.0, -0.5, -1.0, -1.5, -2.0, -3.0, -4.0, -6.0])


def pack_weight(w, fmt):
    k, n = w.shape
    w = f64(np.asarray(w, np.float32).astype(ml_dtypes.bfloat16)).reshape(k // 32, 32, n)
    amax = np.abs(w).max(1)
    if fmt == "e4m3":
        byte = np.frexp(amax)[1] - 1 + 127 - 7
    else:
        mant, ex = np.frexp(amax / 6.0)
        byte = np.where(mant > 0.5, ex, ex - 1) + 127
    byte = np.clip(np.where(amax > 0, byte, 1), 1, 254)
    scaled = (w * np.exp2(127.0 - byte)[:, None, :]).reshape(k, n).astype(np.float32)
    by_word = np.ascontiguousarray(scaled.reshape(k // 512, 128, 4, n).transpose(0, 1, 3, 2))
    if fmt == "e4m3":
        words = by_word.astype(ml_dtypes.float8_e4m3fn).view(np.uint8)
    else:
        c = by_word.astype(ml_dtypes.float4_e2m1fn).view(np.uint8) & 0xF
        words = (c[..., 0::2] | (c[..., 1::2] << 4)).reshape(k // 512, 128, 2 * n)
    return np.ascontiguousarray(words), np.ascontiguousarray(byte.astype(np.uint8).reshape(k // 512, 16, n))


def unpack_weight(words, scales, fmt):
    g, _, n = scales.shape
    words = np.ascontiguousarray(words).reshape(g, 128, n, -1)
    if fmt == "e4m3":
        vals = words.view(ml_dtypes.float8_e4m3fn).astype(np.float64)
    else:
        nib = np.empty((g, 128, n, 4), np.uint8)
        nib[..., 0::2] = words & 0xF
        nib[..., 1::2] = words >> 4
        vals = E2M1[nib]
    vals = vals * np.repeat(np.exp2(scales.astype(np.float64) - 127.0), 8, axis=1)[..., None]
    return vals.transpose(0, 1, 3, 2).reshape(g * 512, n)


def sigmoid(v):
    return 1.0 / (1.0 + np.exp(-v))


D, E, T, I, Q = 512, 512, 2048, 512, 128


def setup_inputs():
    n = np.random.standard_normal
    idx = np.random.permutation(T)[:I]
    fd = mx_kscale(D)
    fe = mx_kscale(E)
    keysp = pack_weight(n((D, T)) / fd[:, None], "e4m3")
    valsp = pack_weight(n((E, T)) / fe[:, None], "e4m3")
    return {
        "query": (n((D, Q)) * 0.8 / np.sqrt(D) * fd[:, None]).astype(np.float32),
        "keys_words": keysp[0],
        "keys_scales": keysp[1],
        "th": (np.random.uniform(0.4, 1.0, (Q, 1))).astype(np.float32),
        "gout": (n((E, Q)) * 1 / np.sqrt(E) * fe[:, None]).astype(np.float32),
        "vals_words": valsp[0],
        "vals_scales": valsp[1],
        "old": (0.5 * n((Q, T))).astype(np.float32),
        "offs": striped(idx),
    }


def reference(query, keys_words, keys_scales, th, gout, vals_words, vals_scales, old, offs):
    idx = unstriped(offs)
    keysu = unpack_weight(keys_words, keys_scales, "e4m3")
    valsu = unpack_weight(vals_words, vals_scales, "e4m3")
    queryq = mxq(f64(query), 0, "e4m3")
    keysidxg = keysu[:, idx]
    a = queryq.T @ keysidxg
    e1s = sigmoid((f64(th) - np.mean(np.square(a), axis=1, keepdims=True)) * 4.0)
    p = np.exp(a - np.max(a, axis=1, keepdims=True))
    z = np.sum(p, axis=1, keepdims=True)
    goutq = mxq(f64(gout), 0, "e4m3")
    valsidxg = valsu[:, idx]
    c0 = goutq.T @ valsidxg
    dz = np.sum(c0 * (1.0 - e1s) * p / np.square(z) * (-1.0), axis=1, keepdims=True)
    dp = c0 * (1.0 - e1s) / z + dz
    de1s = np.sum(c0, axis=1, keepdims=True) / 512.0 - np.sum(c0 * p / z, axis=1, keepdims=True)
    da = dp * p + de1s * e1s * (1.0 - e1s) * 4.0 * (-1.0) / 512.0 * a * 2.0
    gs = da * 512.0
    gf = np.zeros((Q, T))
    gf[:, idx] = gs
    y = f64(old) + gf
    return y

@@ -1,0 +1,159 @@
+from contextlib import ExitStack
+
+import concourse.mybir as mybir
+
+D, E, T, I, Q = 512, 512, 2048, 512, 128
+FLOPS = 2 * 2 * 512 * Q * I
+
+F32 = mybir.dt.float32
+BF16 = mybir.dt.bfloat16
+I32 = mybir.dt.int32
+U32 = mybir.dt.uint32
+U16 = mybir.dt.uint16
+U8 = mybir.dt.uint8
+FP8X4 = mybir.dt.float8_e4m3fn_x4
+ALU = mybir.AluOpType
+ACT = mybir.ActivationFunctionType
+
+P = 128
+HALF = I // 2
+VAL_ROW = 4
+STORE_COLS = (256, 512, 512, 512, 256)
+
+
+def tile_attend_bevenbyspread_s_kernel(tc, query, keys_words, keys_scales, th, gout, vals_words, vals_scales, old, offs, out):
+    nc = tc.nc
+    with ExitStack() as ctx:
+        sb = ctx.enter_context(tc.tile_pool(name="sb", bufs=1))
+        ps = ctx.enter_context(tc.psum_pool(name="ps", bufs=1))
+
+        offsets = sb.tile([P, I // 16], U16, name="offsets")
+        q_raw = sb.tile([P, 4, Q], F32, name="q_raw")
+        g_raw = sb.tile([P, 4, Q], F32, name="g_raw")
+        th_sb = sb.tile([P, 1], F32, name="th_sb")
+        k_pool = sb.tile([P, T], I32, name="k_pool")
+        v_pool = sb.tile([P, T], I32, name="v_pool")
+        ks_pool = sb.tile([P, T], U8, name="ks_pool")
+        vs_pool = sb.tile([P, T], U8, name="vs_pool")
+        old_sb = sb.tile([P, T], F32, name="old_sb")
+        window = sb.tile([P, T], F32, name="window")
+        weights = sb.tile([P, 4], F32, name="weights")
+
+        def load_scales(queue, tile, scales, row):
+            for quad in range(4):
+                queue.dma_start(
+                    tile[32 * quad + row : 32 * quad + row + 4, :].bitcast(I32),
+                    scales[0, 4 * quad : 4 * quad + 4, :].bitcast(I32),
+                )
+
+        def load_words(tile, words):
+            nc.sync.dma_start(tile[:], words[0].rearrange("p n t -> p (n t)").bitcast(I32))
+
+        nc.vector.memset(ks_pool[:, 0:1280].bitcast(I32), 0)
+        nc.gpsimd.memset(ks_pool[:, 1280:T].bitcast(I32), 0)
+        nc.vector.memset(vs_pool[:].bitcast(I32), 0)
+        nc.vector.memset(window[:], 0.0)
+        nc.vector.memset(weights[:, 2:4], 1.0)
+
+        nc.sync.dma_start(offsets[:], offs)
+        nc.sync.dma_start(q_raw[:], query.rearrange("(p j) q -> p j q", j=4))
+        nc.sync.dma_start(th_sb[:], th)
+        load_scales(nc.sync, ks_pool, keys_scales, 0)
+        load_words(k_pool, keys_words)
+        nc.sync.dma_start(g_raw[:], gout.rearrange("(p j) q -> p j q", j=4))
+        load_scales(nc.sync, vs_pool, vals_scales, VAL_ROW)
+        load_words(v_pool, vals_words)
+        nc.sync.dma_start(old_sb[:], old)
+
+        def quantize(raw, name):
+            grouped = sb.tile([P, Q, 4], BF16, name=name + "_bf", align_bytes=64)
+            codes = sb.tile([P, Q], U32, name=name + "_codes", align_bytes=64)
+            scales = sb.tile([P, Q], U8, name=name + "_scales", align_bytes=64)
+            nc.scalar.copy(grouped[:], raw[:].rearrange("p j q -> p q j"))
+            nc.vector.quantize_mx(out=codes[:].bitcast(FP8X4), scales=scales[:], in_=grouped[:].rearrange("p q j -> p (q j)"))
+            return codes, scales
+
+        def gather_scales(pool, name):
+            picked = sb.tile([P, I], U8, name=name, align_bytes=64)
+            nc.vector.tensor_copy(picked[:], pool[:].indirect(offsets[:]))
+            return picked
+
+        def gather_words(pool, h, name):
+            picked = sb.tile([P, HALF], U32, name=name, align_bytes=64)
+            nc.vector.tensor_copy(picked[:], pool[:].bitcast(U32).indirect(offsets[:, 16 * h : 16 * (h + 1)]))
+            return picked
+
+        def product(codes, scales, words, plane, name):
+            bank = ps.tile([P, HALF], F32, name=name)
+            nc.tensor.matmul_mx(out=bank[:], lhsT=codes[:].bitcast(FP8X4), lhsT_scale=scales[:],
+                                rhs=words[:].bitcast(FP8X4), rhs_scale=plane, start=True, stop=True)
+            return bank
+
+        def column(name):
+            return sb.tile([P, 1], F32, name=name)
+
+        halves = [slice(h * HALF, (h + 1) * HALF) for h in range(2)]
+
+        ks = gather_scales(ks_pool, "ks")
+        q_codes, q_scales = quantize(q_raw, "q")
+        th2 = column("th2")
+        nc.scalar.activation(th2[:], th_sb[:], ACT.Identity, scale=-2.0)
+        kw = [gather_words(k_pool, h, "kw%d" % h) for h in range(2)]
+        a = [product(q_codes, q_scales, kw[h], ks[:, halves[h]], "a%d" % h) for h in range(2)]
+
+        neg_a = sb.tile([P, I], F32, name="neg_a")
+        neg_max = [column("neg_max0"), column("neg_max1")]
+        nc.vector.tensor_scalar(neg_a[:, halves[0]], a[0][:], -1.0, None, ALU.mult, ALU.min, accum_out=neg_max[0][:])
+        nc.vector.tensor_scalar(neg_a[:, halves[1]], a[1][:], -1.0, neg_max[0][:], ALU.mult, ALU.min, accum_out=neg_max[1][:])
+
+        vs = gather_scales(vs_pool, "vs")
+        g_codes, g_scales = quantize(g_raw, "g")
+        p = sb.tile([P, I], F32, name="p")
+        z = column("z")
+        nc.scalar.activation(p[:], neg_a[:], ACT.Exp, bias=neg_max[1][:], scale=-1.0, accum_out=z[:])
+        squares = sb.tile([P, I], F32, name="squares")
+        ss = column("ss")
+        nc.scalar.activation(squares[:], neg_a[:], ACT.Square, scale=1.0 / 16, accum_out=ss[:])
+        rz = column("rz")
+        nc.vector.reciprocal(rz[:], z[:])
+        tn = column("tn")
+        nc.scalar.activation(tn[:], ss[:], ACT.Tanh, bias=th2[:])
+        g0 = column("g0")
+        nc.scalar.activation(g0[:], tn[:], ACT.Identity, bias=-256.0, scale=-256.0)
+        gain = column("gain")
+        nc.scalar.activation(gain[:], rz[:], ACT.Identity, scale=g0[:])
+        nc.scalar.activation(weights[:, 0:2], tn[:].to_broadcast([P, 2]), ACT.Identity, bias=1.0 / 128, scale=-1.0 / 128)
+        tn2 = column("tn2")
+        nc.scalar.activation(tn2[:], tn[:], ACT.Square, scale=1.0 / 16)
+        kk = column("kk")
+        nc.scalar.activation(kk[:], tn2[:], ACT.Identity, bias=1.0 / 256, scale=-1.0)
+
+        vw = [gather_words(v_pool, h, "vw%d" % h) for h in range(2)]
+        c = [product(g_codes, g_scales, vw[h], vs[VAL_ROW:P, halves[h]], "c%d" % h) for h in range(2)]
+        c_again = product(g_codes, g_scales, vw[1], vs[VAL_ROW:P, halves[1]], "c_again")
+
+        parts = sb.tile([P, 4], F32, name="parts")
+        t = sb.tile([P, I], F32, name="t")
+        scaled_c = sb.tile([P, I], F32, name="scaled_c")
+        nc.scalar.activation(scaled_c[:, halves[0]], c[0][:], ACT.Identity, scale=kk[:], accum_out=parts[:, 2:3])
+        nc.scalar.activation(scaled_c[:, halves[1]], c_again[:], ACT.Identity, scale=kk[:], accum_out=parts[:, 3:4])
+        for h in range(2):
+            nc.vector.scalar_tensor_tensor(t[:, halves[h]], c[h][:], gain[:], p[:, halves[h]], ALU.mult, ALU.mult, accum_out=parts[:, h : h + 1])
+
+        coef_p = column("coef_p")
+        nc.vector.tensor_scalar(coef_p[:], parts[:, 0:1], parts[:, 1:2], rz[:], ALU.add, ALU.mult)
+        terms = sb.tile([P, 4], F32, name="terms")
+        coef_a = column("coef_a")
+        nc.vector.scalar_tensor_tensor(terms[:], parts[:], 1.0, weights[:], ALU.mult, ALU.mult, accum_out=coef_a[:])
+        w = sb.tile([P, I], F32, name="w")
+        nc.vector.scalar_tensor_tensor(w[:], p[:], coef_p[:], t[:], ALU.mult, ALU.subtract)
+        v = sb.tile([P, I], F32, name="v")
+        nc.scalar.activation(v[:], neg_a[:], ACT.Identity, scale=coef_a[:])
+        nc.vector.tensor_tensor(window[:].indirect(offsets[:]), w[:], v[:], ALU.add)
+
+        start = 0
+        for width in STORE_COLS:
+            cols = slice(start, start + width)
+            nc.vector.tensor_tensor(old_sb[:, cols], old_sb[:, cols], window[:, cols], ALU.add)
+            nc.sync.dma_start(out[:, cols], old_sb[:, cols])
+            start = start + width

@@ -18,7 +18,7 @@ ACT = mybir.ActivationFunctionType
 P = 128
 HALF = I // 2
 VAL_ROW = 4
-STORE_COLS = (256, 512, 512, 512, 256)
+STORE_COLS = (128, 384, 512, 512, 384, 128)
 
 
 def tile_attend_bevenbyspread_s_kernel(tc, query, keys_words, keys_scales, th, gout, vals_words, vals_scales, old, offs, out):
@@ -29,15 +29,11 @@ def tile_attend_bevenbyspread_s_kernel(tc, query, keys_words, keys_scales, th, g
 
         offsets = sb.tile([P, I // 16], U16, name="offsets")
         q_raw = sb.tile([P, 4, Q], F32, name="q_raw")
-        g_raw = sb.tile([P, 4, Q], F32, name="g_raw")
+        g_raw = sb.tile([P, 4, Q], F32, name="g_raw", tag="g_then_p")
         th_sb = sb.tile([P, 1], F32, name="th_sb")
-        k_pool = sb.tile([P, T], I32, name="k_pool")
-        v_pool = sb.tile([P, T], I32, name="v_pool")
         ks_pool = sb.tile([P, T], U8, name="ks_pool")
-        vs_pool = sb.tile([P, T], U8, name="vs_pool")
-        old_sb = sb.tile([P, T], F32, name="old_sb")
+        vs_pool = sb.tile([P, T], U8, name="vs_pool", tag="vs_then_neg_a")
         window = sb.tile([P, T], F32, name="window")
-        weights = sb.tile([P, 4], F32, name="weights")
 
         def load_scales(queue, tile, scales, row):
             for quad in range(4):
@@ -49,43 +45,46 @@ def tile_attend_bevenbyspread_s_kernel(tc, query, keys_words, keys_scales, th, g
         def load_words(tile, words):
             nc.sync.dma_start(tile[:], words[0].rearrange("p n t -> p (n t)").bitcast(I32))
 
+        k_pool = sb.tile([P, T], I32, name="k_pool")
+        v_pool = sb.tile([P, T], I32, name="v_pool", tag="v_then_rz")
+        old_sb = sb.tile([P, T], F32, name="old_sb")
+
         nc.vector.memset(ks_pool[:, 0:1280].bitcast(I32), 0)
         nc.gpsimd.memset(ks_pool[:, 1280:T].bitcast(I32), 0)
         nc.vector.memset(vs_pool[:].bitcast(I32), 0)
         nc.vector.memset(window[:], 0.0)
-        nc.vector.memset(weights[:, 2:4], 1.0)
 
         nc.sync.dma_start(offsets[:], offs)
         nc.sync.dma_start(q_raw[:], query.rearrange("(p j) q -> p j q", j=4))
         nc.sync.dma_start(th_sb[:], th)
         load_scales(nc.sync, ks_pool, keys_scales, 0)
         load_words(k_pool, keys_words)
-        nc.sync.dma_start(g_raw[:], gout.rearrange("(p j) q -> p j q", j=4))
         load_scales(nc.sync, vs_pool, vals_scales, VAL_ROW)
+        nc.sync.dma_start(g_raw[:], gout.rearrange("(p j) q -> p j q", j=4))
         load_words(v_pool, vals_words)
         nc.sync.dma_start(old_sb[:], old)
 
         def quantize(raw, name):
-            grouped = sb.tile([P, Q, 4], BF16, name=name + "_bf", align_bytes=64)
+            grouped = sb.tile([P, Q, 4], BF16, name=name + "_bf", tag=name + "_bf", align_bytes=64)
             codes = sb.tile([P, Q], U32, name=name + "_codes", align_bytes=64)
-            scales = sb.tile([P, Q], U8, name=name + "_scales", align_bytes=64)
+            plane = sb.tile([P, Q], U8, name=name + "_plane", align_bytes=64)
             nc.scalar.copy(grouped[:], raw[:].rearrange("p j q -> p q j"))
-            nc.vector.quantize_mx(out=codes[:].bitcast(FP8X4), scales=scales[:], in_=grouped[:].rearrange("p q j -> p (q j)"))
-            return codes, scales
+            nc.vector.quantize_mx(out=codes[:].bitcast(FP8X4), scales=plane[:], in_=grouped[:].rearrange("p q j -> p (q j)"))
+            return codes[:], plane[:]
 
         def gather_scales(pool, name):
             picked = sb.tile([P, I], U8, name=name, align_bytes=64)
             nc.vector.tensor_copy(picked[:], pool[:].indirect(offsets[:]))
             return picked
 
-        def gather_words(pool, h, name):
-            picked = sb.tile([P, HALF], U32, name=name, align_bytes=64)
-            nc.vector.tensor_copy(picked[:], pool[:].bitcast(U32).indirect(offsets[:, 16 * h : 16 * (h + 1)]))
+        def gather_words(pool, slots, name):
+            picked = sb.tile([P, slots.stop - slots.start], U32, name=name, align_bytes=64)
+            nc.vector.tensor_copy(picked[:], pool[:].bitcast(U32).indirect(offsets[:, slots.start // 16 : slots.stop // 16]))
             return picked
 
-        def product(codes, scales, words, plane, name):
-            bank = ps.tile([P, HALF], F32, name=name)
-            nc.tensor.matmul_mx(out=bank[:], lhsT=codes[:].bitcast(FP8X4), lhsT_scale=scales[:],
+        def product(lhs, lhs_plane, words, plane, name):
+            bank = ps.tile([P, words.shape[1]], F32, name=name)
+            nc.tensor.matmul_mx(out=bank[:], lhsT=lhs.bitcast(FP8X4), lhsT_scale=lhs_plane,
                                 rhs=words[:].bitcast(FP8X4), rhs_scale=plane, start=True, stop=True)
             return bank
 
@@ -98,62 +97,64 @@ def tile_attend_bevenbyspread_s_kernel(tc, query, keys_words, keys_scales, th, g
         q_codes, q_scales = quantize(q_raw, "q")
         th2 = column("th2")
         nc.scalar.activation(th2[:], th_sb[:], ACT.Identity, scale=-2.0)
-        kw = [gather_words(k_pool, h, "kw%d" % h) for h in range(2)]
-        a = [product(q_codes, q_scales, kw[h], ks[:, halves[h]], "a%d" % h) for h in range(2)]
-
-        neg_a = sb.tile([P, I], F32, name="neg_a")
-        neg_max = [column("neg_max0"), column("neg_max1")]
-        nc.vector.tensor_scalar(neg_a[:, halves[0]], a[0][:], -1.0, None, ALU.mult, ALU.min, accum_out=neg_max[0][:])
-        nc.vector.tensor_scalar(neg_a[:, halves[1]], a[1][:], -1.0, neg_max[0][:], ALU.mult, ALU.min, accum_out=neg_max[1][:])
-
+        kw = gather_words(k_pool, slice(0, I), "kw")
+        a = product(q_codes, q_scales, kw, ks[:], "a")
         vs = gather_scales(vs_pool, "vs")
+
+        neg_a = sb.tile([P, I], F32, name="neg_a", tag="vs_then_neg_a")
+        neg_max = column("neg_max")
+        nc.vector.tensor_scalar(neg_a[:], a[:], -1.0, None, ALU.mult, ALU.min, accum_out=neg_max[:])
         g_codes, g_scales = quantize(g_raw, "g")
-        p = sb.tile([P, I], F32, name="p")
+        p = sb.tile([P, I], F32, name="p", tag="g_then_p")
         z = column("z")
-        nc.scalar.activation(p[:], neg_a[:], ACT.Exp, bias=neg_max[1][:], scale=-1.0, accum_out=z[:])
-        squares = sb.tile([P, I], F32, name="squares")
+        nc.scalar.activation(p[:], neg_a[:], ACT.Exp, bias=neg_max[:], scale=-1.0, accum_out=z[:])
+        squares = sb.tile([P, I], F32, name="squares", tag="g_bf", align_bytes=64)
         ss = column("ss")
         nc.scalar.activation(squares[:], neg_a[:], ACT.Square, scale=1.0 / 16, accum_out=ss[:])
-        rz = column("rz")
-        nc.vector.reciprocal(rz[:], z[:])
         tn = column("tn")
         nc.scalar.activation(tn[:], ss[:], ACT.Tanh, bias=th2[:])
         g0 = column("g0")
         nc.scalar.activation(g0[:], tn[:], ACT.Identity, bias=-256.0, scale=-256.0)
-        gain = column("gain")
-        nc.scalar.activation(gain[:], rz[:], ACT.Identity, scale=g0[:])
-        nc.scalar.activation(weights[:, 0:2], tn[:].to_broadcast([P, 2]), ACT.Identity, bias=1.0 / 128, scale=-1.0 / 128)
-        tn2 = column("tn2")
-        nc.scalar.activation(tn2[:], tn[:], ACT.Square, scale=1.0 / 16)
-        kk = column("kk")
-        nc.scalar.activation(kk[:], tn2[:], ACT.Identity, bias=1.0 / 256, scale=-1.0)
 
-        vw = [gather_words(v_pool, h, "vw%d" % h) for h in range(2)]
+        vw = [gather_words(v_pool, halves[h], "vw%d" % h) for h in range(2)]
         c = [product(g_codes, g_scales, vw[h], vs[VAL_ROW:P, halves[h]], "c%d" % h) for h in range(2)]
         c_again = product(g_codes, g_scales, vw[1], vs[VAL_ROW:P, halves[1]], "c_again")
 
-        parts = sb.tile([P, 4], F32, name="parts")
+        factors = sb.tile([P, 2], F32, name="factors", tag="v_then_rz")
+        rz = factors[:, 0:1]
+        e64 = factors[:, 1:2]
+        nc.vector.reciprocal(rz, z[:])
+        nc.scalar.activation(e64, tn[:], ACT.Identity, bias=1.0 / 128, scale=-1.0 / 128)
+        ez = column("ez")
+        nc.scalar.activation(ez[:], e64, ACT.Identity, scale=z[:])
+        m = [column("m0"), column("m1")]
         t = sb.tile([P, I], F32, name="t")
+        first_terms = sb.tile([P, 2], F32, name="first_terms")
+        terms = sb.tile([P, 2], F32, name="terms")
+        nc.vector.scalar_tensor_tensor(t[:, halves[0]], c[0][:], 1.0, p[:, halves[0]], ALU.mult, ALU.mult, accum_out=m[0][:])
+        nc.vector.tensor_scalar(first_terms[:], factors[:], m[0][:], None, ALU.mult)
+        nc.vector.scalar_tensor_tensor(t[:, halves[1]], c[1][:], 1.0, p[:, halves[1]], ALU.mult, ALU.mult, accum_out=m[1][:])
+        nc.vector.scalar_tensor_tensor(terms[:], factors[:], m[1][:], first_terms[:], ALU.mult, ALU.add)
         scaled_c = sb.tile([P, I], F32, name="scaled_c")
-        nc.scalar.activation(scaled_c[:, halves[0]], c[0][:], ACT.Identity, scale=kk[:], accum_out=parts[:, 2:3])
-        nc.scalar.activation(scaled_c[:, halves[1]], c_again[:], ACT.Identity, scale=kk[:], accum_out=parts[:, 3:4])
-        for h in range(2):
-            nc.vector.scalar_tensor_tensor(t[:, halves[h]], c[h][:], gain[:], p[:, halves[h]], ALU.mult, ALU.mult, accum_out=parts[:, h : h + 1])
+        s_share = column("s_share")
+        s_all = column("s_all")
+        nc.scalar.activation(scaled_c[:, halves[0]], c[0][:], ACT.Identity, scale=-1.0 / (I * HALF), accum_out=s_share[:])
+        nc.scalar.activation(scaled_c[:, halves[1]], c_again[:], ACT.Identity, scale=-1.0 / I, bias=s_share[:], accum_out=s_all[:])
 
-        coef_p = column("coef_p")
-        nc.vector.tensor_scalar(coef_p[:], parts[:, 0:1], parts[:, 1:2], rz[:], ALU.add, ALU.mult)
-        terms = sb.tile([P, 4], F32, name="terms")
-        coef_a = column("coef_a")
-        nc.vector.scalar_tensor_tensor(terms[:], parts[:], 1.0, weights[:], ALU.mult, ALU.mult, accum_out=coef_a[:])
         w = sb.tile([P, I], F32, name="w")
-        nc.vector.scalar_tensor_tensor(w[:], p[:], coef_p[:], t[:], ALU.mult, ALU.subtract)
+        nc.vector.scalar_tensor_tensor(w[:], p[:], terms[:, 0:1], t[:], ALU.mult, ALU.subtract)
+        coef_a = column("coef_a")
+        nc.scalar.activation(coef_a[:], s_all[:], ACT.Identity, scale=ez[:], bias=terms[:, 1:2])
         v = sb.tile([P, I], F32, name="v")
         nc.scalar.activation(v[:], neg_a[:], ACT.Identity, scale=coef_a[:])
         nc.vector.tensor_tensor(window[:].indirect(offsets[:]), w[:], v[:], ALU.add)
 
+        gain = column("gain")
+        nc.scalar.activation(gain[:], rz, ACT.Identity, scale=g0[:])
+
         start = 0
         for width in STORE_COLS:
             cols = slice(start, start + width)
-            nc.vector.tensor_tensor(old_sb[:, cols], old_sb[:, cols], window[:, cols], ALU.add)
+            nc.vector.scalar_tensor_tensor(old_sb[:, cols], window[:, cols], gain[:], old_sb[:, cols], ALU.mult, ALU.add)
             nc.sync.dma_start(out[:, cols], old_sb[:, cols])
             start = start + width

@@ -32,7 +32,7 @@ def tile_attend_bevenbyspread_s_kernel(tc, query, keys_words, keys_scales, th, g
         g_raw = sb.tile([P, 4, Q], F32, name="g_raw", tag="g_then_p")
         th_sb = sb.tile([P, 1], F32, name="th_sb")
         ks_pool = sb.tile([P, T], U8, name="ks_pool")
-        vs_pool = sb.tile([P, T], U8, name="vs_pool", tag="vs_then_neg_a")
+        vs_pool = sb.tile([P, T], U8, name="vs_pool", tag="vs_then_old")
         window = sb.tile([P, T], F32, name="window")
 
         def load_scales(queue, tile, scales, row):
@@ -47,22 +47,22 @@ def tile_attend_bevenbyspread_s_kernel(tc, query, keys_words, keys_scales, th, g
 
         k_pool = sb.tile([P, T], I32, name="k_pool")
         v_pool = sb.tile([P, T], I32, name="v_pool", tag="v_then_rz")
-        old_sb = sb.tile([P, T], F32, name="old_sb")
+        vs = sb.tile([P, I], U8, name="vs", align_bytes=64)
 
         nc.vector.memset(ks_pool[:, 0:1280].bitcast(I32), 0)
         nc.gpsimd.memset(ks_pool[:, 1280:T].bitcast(I32), 0)
-        nc.vector.memset(vs_pool[:].bitcast(I32), 0)
+        nc.vector.memset(vs[:].bitcast(I32), 0)
         nc.vector.memset(window[:], 0.0)
+        nc.gpsimd.memset(vs_pool[0:112, :].bitcast(I32), 0)
 
         nc.sync.dma_start(offsets[:], offs)
         nc.sync.dma_start(q_raw[:], query.rearrange("(p j) q -> p j q", j=4))
-        nc.sync.dma_start(th_sb[:], th)
+        nc.sync.dma_start(vs_pool[112:P, :].bitcast(I32), vals_scales[0].bitcast(I32))
         load_scales(nc.sync, ks_pool, keys_scales, 0)
         load_words(k_pool, keys_words)
-        load_scales(nc.sync, vs_pool, vals_scales, VAL_ROW)
         nc.sync.dma_start(g_raw[:], gout.rearrange("(p j) q -> p j q", j=4))
         load_words(v_pool, vals_words)
-        nc.sync.dma_start(old_sb[:], old)
+        nc.sync.dma_start(th_sb[:], th)
 
         def quantize(raw, name):
             grouped = sb.tile([P, Q, 4], BF16, name=name + "_bf", tag=name + "_bf", align_bytes=64)
@@ -95,15 +95,22 @@ def tile_attend_bevenbyspread_s_kernel(tc, query, keys_words, keys_scales, th, g
 
         ks = gather_scales(ks_pool, "ks")
         q_codes, q_scales = quantize(q_raw, "q")
-        th2 = column("th2")
-        nc.scalar.activation(th2[:], th_sb[:], ACT.Identity, scale=-2.0)
-        kw = gather_words(k_pool, slice(0, I), "kw")
-        a = product(q_codes, q_scales, kw, ks[:], "a")
-        vs = gather_scales(vs_pool, "vs")
+        vs_rows = gather_scales(vs_pool, "vs_rows")
+        for quad in range(4):
+            nc.sync.dma_start(
+                vs[32 * quad + VAL_ROW : 32 * quad + VAL_ROW + 4, :].bitcast(I32),
+                vs_rows[112 + 4 * quad : 116 + 4 * quad, :].bitcast(I32),
+            )
+        old_sb = sb.tile([P, T], F32, name="old_sb", tag="vs_then_old")
+        nc.sync.dma_start(old_sb[:], old)
+        kw = [gather_words(k_pool, halves[h], "kw%d" % h) for h in range(2)]
+        a = [product(q_codes, q_scales, kw[h], ks[:, halves[h]], "a%d" % h) for h in range(2)]
 
-        neg_a = sb.tile([P, I], F32, name="neg_a", tag="vs_then_neg_a")
+        neg_a = sb.tile([P, I], F32, name="neg_a")
         neg_max = column("neg_max")
-        nc.vector.tensor_scalar(neg_a[:], a[:], -1.0, None, ALU.mult, ALU.min, accum_out=neg_max[:])
+        neg_max_half = column("neg_max_half")
+        nc.vector.tensor_scalar(neg_a[:, halves[0]], a[0][:], -1.0, None, ALU.mult, ALU.min, accum_out=neg_max_half[:])
+        nc.vector.tensor_scalar(neg_a[:, halves[1]], a[1][:], -1.0, neg_max_half[:], ALU.mult, ALU.min, accum_out=neg_max[:])
         g_codes, g_scales = quantize(g_raw, "g")
         p = sb.tile([P, I], F32, name="p", tag="g_then_p")
         z = column("z")
@@ -112,7 +119,7 @@ def tile_attend_bevenbyspread_s_kernel(tc, query, keys_words, keys_scales, th, g
         ss = column("ss")
         nc.scalar.activation(squares[:], neg_a[:], ACT.Square, scale=1.0 / 16, accum_out=ss[:])
         tn = column("tn")
-        nc.scalar.activation(tn[:], ss[:], ACT.Tanh, bias=th2[:])
+        nc.scalar.activation(tn[:], th_sb[:], ACT.Tanh, bias=ss[:], scale=-2.0)
         g0 = column("g0")
         nc.scalar.activation(g0[:], tn[:], ACT.Identity, bias=-256.0, scale=-256.0)
 

from contextlib import ExitStack

import concourse.mybir as mybir

D, E, T, I, Q = 512, 512, 2048, 512, 128
FLOPS = 2 * 2 * 512 * Q * I

F32 = mybir.dt.float32
BF16 = mybir.dt.bfloat16
I32 = mybir.dt.int32
U32 = mybir.dt.uint32
U16 = mybir.dt.uint16
U8 = mybir.dt.uint8
FP8X4 = mybir.dt.float8_e4m3fn_x4
ALU = mybir.AluOpType
ACT = mybir.ActivationFunctionType

P = 128
HALF = I // 2
VAL_ROW = 4
STORE_COLS = (128, 384, 512, 512, 384, 128)


def tile_attend_bevenbyspread_s_kernel(tc, query, keys_words, keys_scales, th, gout, vals_words, vals_scales, old, offs, out):
    nc = tc.nc
    with ExitStack() as ctx:
        sb = ctx.enter_context(tc.tile_pool(name="sb", bufs=1))
        ps = ctx.enter_context(tc.psum_pool(name="ps", bufs=1))

        offsets = sb.tile([P, I // 16], U16, name="offsets")
        q_raw = sb.tile([P, 4, Q], F32, name="q_raw")
        g_raw = sb.tile([P, 4, Q], F32, name="g_raw", tag="g_then_p")
        th_sb = sb.tile([P, 1], F32, name="th_sb")
        ks_pool = sb.tile([P, T], U8, name="ks_pool")
        vs_pool = sb.tile([P, T], U8, name="vs_pool", tag="vs_then_old")
        window = sb.tile([P, T], F32, name="window")

        def load_scales(queue, tile, scales, row):
            for quad in range(4):
                queue.dma_start(
                    tile[32 * quad + row : 32 * quad + row + 4, :].bitcast(I32),
                    scales[0, 4 * quad : 4 * quad + 4, :].bitcast(I32),
                )

        def load_words(tile, words):
            nc.sync.dma_start(tile[:], words[0].rearrange("p n t -> p (n t)").bitcast(I32))

        k_pool = sb.tile([P, T], I32, name="k_pool")
        v_pool = sb.tile([P, T], I32, name="v_pool", tag="v_then_rz")
        vs = sb.tile([P, I], U8, name="vs", align_bytes=64)

        nc.vector.memset(ks_pool[:, 0:1280].bitcast(I32), 0)
        nc.gpsimd.memset(ks_pool[:, 1280:T].bitcast(I32), 0)
        nc.vector.memset(vs[:].bitcast(I32), 0)
        nc.vector.memset(window[:], 0.0)
        nc.gpsimd.memset(vs_pool[0:112, :].bitcast(I32), 0)

        nc.sync.dma_start(offsets[:], offs)
        nc.sync.dma_start(q_raw[:], query.rearrange("(p j) q -> p j q", j=4))
        nc.sync.dma_start(vs_pool[112:P, :].bitcast(I32), vals_scales[0].bitcast(I32))
        load_scales(nc.sync, ks_pool, keys_scales, 0)
        load_words(k_pool, keys_words)
        nc.sync.dma_start(g_raw[:], gout.rearrange("(p j) q -> p j q", j=4))
        load_words(v_pool, vals_words)
        nc.sync.dma_start(th_sb[:], th)

        def quantize(raw, name):
            grouped = sb.tile([P, Q, 4], BF16, name=name + "_bf", tag=name + "_bf", align_bytes=64)
            codes = sb.tile([P, Q], U32, name=name + "_codes", align_bytes=64)
            plane = sb.tile([P, Q], U8, name=name + "_plane", align_bytes=64)
            nc.scalar.copy(grouped[:], raw[:].rearrange("p j q -> p q j"))
            nc.vector.quantize_mx(out=codes[:].bitcast(FP8X4), scales=plane[:], in_=grouped[:].rearrange("p q j -> p (q j)"))
            return codes[:], plane[:]

        def gather_scales(pool, name):
            picked = sb.tile([P, I], U8, name=name, align_bytes=64)
            nc.vector.tensor_copy(picked[:], pool[:].indirect(offsets[:]))
            return picked

        def gather_words(pool, slots, name):
            picked = sb.tile([P, slots.stop - slots.start], U32, name=name, align_bytes=64)
            nc.vector.tensor_copy(picked[:], pool[:].bitcast(U32).indirect(offsets[:, slots.start // 16 : slots.stop // 16]))
            return picked

        def product(lhs, lhs_plane, words, plane, name):
            bank = ps.tile([P, words.shape[1]], F32, name=name)
            nc.tensor.matmul_mx(out=bank[:], lhsT=lhs.bitcast(FP8X4), lhsT_scale=lhs_plane,
                                rhs=words[:].bitcast(FP8X4), rhs_scale=plane, start=True, stop=True)
            return bank

        def column(name):
            return sb.tile([P, 1], F32, name=name)

        halves = [slice(h * HALF, (h + 1) * HALF) for h in range(2)]

        ks = gather_scales(ks_pool, "ks")
        q_codes, q_scales = quantize(q_raw, "q")
        vs_rows = gather_scales(vs_pool, "vs_rows")
        for quad in range(4):
            nc.sync.dma_start(
                vs[32 * quad + VAL_ROW : 32 * quad + VAL_ROW + 4, :].bitcast(I32),
                vs_rows[112 + 4 * quad : 116 + 4 * quad, :].bitcast(I32),
            )
        old_sb = sb.tile([P, T], F32, name="old_sb", tag="vs_then_old")
        nc.sync.dma_start(old_sb[:], old)
        kw = [gather_words(k_pool, halves[h], "kw%d" % h) for h in range(2)]
        a = [product(q_codes, q_scales, kw[h], ks[:, halves[h]], "a%d" % h) for h in range(2)]

        neg_a = sb.tile([P, I], F32, name="neg_a")
        neg_max = column("neg_max")
        neg_max_half = column("neg_max_half")
        nc.vector.tensor_scalar(neg_a[:, halves[0]], a[0][:], -1.0, None, ALU.mult, ALU.min, accum_out=neg_max_half[:])
        nc.vector.tensor_scalar(neg_a[:, halves[1]], a[1][:], -1.0, neg_max_half[:], ALU.mult, ALU.min, accum_out=neg_max[:])
        g_codes, g_scales = quantize(g_raw, "g")
        p = sb.tile([P, I], F32, name="p", tag="g_then_p")
        z = column("z")
        nc.scalar.activation(p[:], neg_a[:], ACT.Exp, bias=neg_max[:], scale=-1.0, accum_out=z[:])
        squares = sb.tile([P, I], F32, name="squares", tag="g_bf", align_bytes=64)
        ss = column("ss")
        nc.scalar.activation(squares[:], neg_a[:], ACT.Square, scale=1.0 / 16, accum_out=ss[:])
        tn = column("tn")
        nc.scalar.activation(tn[:], th_sb[:], ACT.Tanh, bias=ss[:], scale=-2.0)
        g0 = column("g0")
        nc.scalar.activation(g0[:], tn[:], ACT.Identity, bias=-256.0, scale=-256.0)

        vw = [gather_words(v_pool, halves[h], "vw%d" % h) for h in range(2)]
        c = [product(g_codes, g_scales, vw[h], vs[VAL_ROW:P, halves[h]], "c%d" % h) for h in range(2)]
        c_again = product(g_codes, g_scales, vw[1], vs[VAL_ROW:P, halves[1]], "c_again")

        factors = sb.tile([P, 2], F32, name="factors", tag="v_then_rz")
        rz = factors[:, 0:1]
        e64 = factors[:, 1:2]
        nc.vector.reciprocal(rz, z[:])
        nc.scalar.activation(e64, tn[:], ACT.Identity, bias=1.0 / 128, scale=-1.0 / 128)
        ez = column("ez")
        nc.scalar.activation(ez[:], e64, ACT.Identity, scale=z[:])
        m = [column("m0"), column("m1")]
        t = sb.tile([P, I], F32, name="t")
        first_terms = sb.tile([P, 2], F32, name="first_terms")
        terms = sb.tile([P, 2], F32, name="terms")
        nc.vector.scalar_tensor_tensor(t[:, halves[0]], c[0][:], 1.0, p[:, halves[0]], ALU.mult, ALU.mult, accum_out=m[0][:])
        nc.vector.tensor_scalar(first_terms[:], factors[:], m[0][:], None, ALU.mult)
        nc.vector.scalar_tensor_tensor(t[:, halves[1]], c[1][:], 1.0, p[:, halves[1]], ALU.mult, ALU.mult, accum_out=m[1][:])
        nc.vector.scalar_tensor_tensor(terms[:], factors[:], m[1][:], first_terms[:], ALU.mult, ALU.add)
        scaled_c = sb.tile([P, I], F32, name="scaled_c")
        s_share = column("s_share")
        s_all = column("s_all")
        nc.scalar.activation(scaled_c[:, halves[0]], c[0][:], ACT.Identity, scale=-1.0 / (I * HALF), accum_out=s_share[:])
        nc.scalar.activation(scaled_c[:, halves[1]], c_again[:], ACT.Identity, scale=-1.0 / I, bias=s_share[:], accum_out=s_all[:])

        w = sb.tile([P, I], F32, name="w")
        nc.vector.scalar_tensor_tensor(w[:], p[:], terms[:, 0:1], t[:], ALU.mult, ALU.subtract)
        coef_a = column("coef_a")
        nc.scalar.activation(coef_a[:], s_all[:], ACT.Identity, scale=ez[:], bias=terms[:, 1:2])
        v = sb.tile([P, I], F32, name="v")
        nc.scalar.activation(v[:], neg_a[:], ACT.Identity, scale=coef_a[:])
        nc.vector.tensor_tensor(window[:].indirect(offsets[:]), w[:], v[:], ALU.add)

        gain = column("gain")
        nc.scalar.activation(gain[:], rz, ACT.Identity, scale=g0[:])

        start = 0
        for width in STORE_COLS:
            cols = slice(start, start + width)
            nc.vector.scalar_tensor_tensor(old_sb[:, cols], window[:, cols], gain[:], old_sb[:, cols], ALU.mult, ALU.add)
            nc.sync.dma_start(out[:, cols], old_sb[:, cols])
            start = start + width
